import numpy as np
import ml_dtypes


def mxq(x, axis, fmt="e4m3"):
    dtype, down = {"e4m3": (ml_dtypes.float8_e4m3fn, 7), "e5m2": (ml_dtypes.float8_e5m2, 14)}[fmt]
    v = np.moveaxis(np.asarray(x, np.float32).astype(ml_dtypes.bfloat16).astype(np.float64), axis, -1)
    blocks = v.reshape(v.shape[:-1] + (-1, 32))
    amax = np.abs(blocks).max(-1, keepdims=True)
    byte = np.maximum(np.where(amax > 0, np.frexp(amax)[1] - 1 + 127, 0) - down, 1)
    scale = np.exp2(byte - 127.0)
    codes = (blocks / scale).astype(np.float32).astype(dtype).astype(np.float64)
    return np.moveaxis((codes * scale).reshape(v.shape), -1, axis)


WIDE = False


def mx_kscale(k):
    if not WIDE:
        return np.ones(k)
    levels = np.array([30, -30])
    if k % 512:
        return np.exp2(np.random.permutation(np.resize(levels, k // 32))).repeat(32)
    a = np.empty((k // 512, 16))
    for p in range(k // 512):
        a[p, :8] = np.random.permutation(np.resize(levels, 8))
        for g in range(8):
            far = levels[np.abs(levels - a[p, g]) >= 10]
            a[p, g + 8] = far[np.random.randint(len(far))]
    return np.exp2(a.ravel()).repeat(32)


def f64(x):
    return np.asarray(x).astype(np.float64)


def striped(idx):
    return np.tile(np.asarray(idx).reshape(-1, 16).T, (8, 1)).astype(np.uint16)


def unstriped(offs):
    return offs[:16].T.reshape(-1).astype(np.int64)


E2M1 = np.array([0.0, 0.5, 1.0, 1.5, 2.0, 3.0, 4.0, 6.0, -0.0, -0.5, -1.0, -1.5, -2.0, -3.0, -4.0, -6.0])


def pack_weight(w, fmt):
    k, n = w.shape
    w = f64(np.asarray(w, np.float32).astype(ml_dtypes.bfloat16)).reshape(k // 32, 32, n)
    amax = np.abs(w).max(1)
    if fmt in ("e4m3", "e5m2"):
        byte = np.frexp(amax)[1] - 1 + 127 - (7 if fmt == "e4m3" else 14)
    else:
        mant, ex = np.frexp(amax / 6.0)
        byte = np.where(mant > 0.5, ex, ex - 1) + 127
    byte = np.clip(np.where(amax > 0, byte, 1), 1, 254)
    scaled = (w * np.exp2(127.0 - byte)[:, None, :]).reshape(k, n).astype(np.float32)
    by_word = np.ascontiguousarray(scaled.reshape(k // 512, 128, 4, n).transpose(0, 1, 3, 2))
    if fmt in ("e4m3", "e5m2"):
        words = by_word.astype(ml_dtypes.float8_e4m3fn if fmt == "e4m3" else ml_dtypes.float8_e5m2).view(np.uint8)
    else:
        c = by_word.astype(ml_dtypes.float4_e2m1fn).view(np.uint8) & 0xF
        words = (c[..., 0::2] | (c[..., 1::2] << 4)).reshape(k // 512, 128, 2 * n)
    return np.ascontiguousarray(words), np.ascontiguousarray(byte.astype(np.uint8).reshape(k // 512, 16, n))


def unpack_weight(words, scales, fmt):
    g, _, n = scales.shape
    words = np.ascontiguousarray(words).reshape(g, 128, n, -1)
    if fmt in ("e4m3", "e5m2"):
        vals = words.view(ml_dtypes.float8_e4m3fn if fmt == "e4m3" else ml_dtypes.float8_e5m2).astype(np.float64)
    else:
        nib = np.empty((g, 128, n, 4), np.uint8)
        nib[..., 0::2] = words & 0xF
        nib[..., 1::2] = words >> 4
        vals = E2M1[nib]
    vals = vals * np.repeat(np.exp2(scales.astype(np.float64) - 127.0), 8, axis=1)[..., None]
    return vals.transpose(0, 1, 3, 2).reshape(g * 512, n)


K, T, Z, J, R, N, L, E = 512, 1024, 1024, 256, 512, 256, 512, 1024


def setup_inputs():
    n = np.random.standard_normal
    idx = np.random.permutation(T)[:J]
    idx2 = np.random.permutation(Z)[:J]
    idx3 = np.random.permutation(E)[:J]
    fk = mx_kscale(K)
    fr = mx_kscale(R)
    fl = mx_kscale(L)
    xtp = pack_weight(n((K, T)) / fk[:, None], "e2m1")
    xop = pack_weight(n((K, Z)) / fk[:, None], "e4m3")
    wp = pack_weight(n((K, R)) * 1 / np.sqrt(K) * fk[:, None] * fr, "e4m3")
    w2p = pack_weight(n((K, R)) * 1 / np.sqrt(K) * fk[:, None] * fr, "e5m2")
    wbp = pack_weight(n((R, N)) * 1 / np.sqrt(R) / fr[:, None], "e2m1")
    sxp = pack_weight(n((L, J)) / fl[:, None], "e4m3")
    wsp = pack_weight(n((L, N)) * 1 / np.sqrt(L) * fl[:, None], "e4m3")
    return {
        "xt_words": xtp[0],
        "xt_scales": xtp[1],
        "xo_words": xop[0],
        "xo_scales": xop[1],
        "w_words": wp[0],
        "w_scales": wp[1],
        "w2_words": w2p[0],
        "w2_scales": w2p[1],
        "wb_words": wbp[0],
        "wb_scales": wbp[1],
        "sx_words": sxp[0],
        "sx_scales": sxp[1],
        "ws_words": wsp[0],
        "ws_scales": wsp[1],
        "tz": (n((N, E))).astype(np.float32),
        "offs": striped(idx),
        "offs2": striped(idx2),
        "offs3": striped(idx3),
    }


def reference(xt_words, xt_scales, xo_words, xo_scales, w_words, w_scales, w2_words, w2_scales, wb_words, wb_scales, sx_words, sx_scales, ws_words, ws_scales, tz, offs, offs2, offs3):
    idx = unstriped(offs)
    idx2 = unstriped(offs2)
    idx3 = unstriped(offs3)
    xtu = unpack_weight(xt_words, xt_scales, "e2m1")
    xou = unpack_weight(xo_words, xo_scales, "e4m3")
    wu = unpack_weight(w_words, w_scales, "e4m3")
    w2u = unpack_weight(w2_words, w2_scales, "e5m2")
    wbu = unpack_weight(wb_words, wb_scales, "e2m1")
    sxu = unpack_weight(sx_words, sx_scales, "e4m3")
    wsu = unpack_weight(ws_words, ws_scales, "e4m3")
    xtidxg = xtu[:, idx]
    xoidx2g = xou[:, idx2]
    a = wu.T @ xtidxg + w2u.T @ xoidx2g
    b = w2u.T @ xtidxg + wu.T @ xoidx2g
    hid = np.maximum(a, b)
    hidq = mxq(hid, 0, "e5m2")
    p = wbu.T @ hidq + wsu.T @ sxu
    y = p + f64(tz)[:, idx3]
    return y

@@ -1,0 +1,176 @@
+from contextlib import ExitStack
+
+import concourse.mybir as mybir
+
+K, T, Z, J, R, N, L, E = 512, 1024, 1024, 256, 512, 256, 512, 1024
+FLOPS = 2 * (4 * K * R * J + R * N * J + L * N * J)
+
+F32 = mybir.dt.float32
+BF16 = mybir.dt.bfloat16
+I32 = mybir.dt.int32
+U32 = mybir.dt.uint32
+U16 = mybir.dt.uint16
+U8 = mybir.dt.uint8
+E4M3 = mybir.dt.float8_e4m3fn_x4
+E5M2 = mybir.dt.float8_e5m2_x4
+E2M1 = mybir.dt.float4_e2m1fn_x4
+COPY = mybir.ActivationFunctionType.Copy
+ADD = mybir.AluOpType.add
+MAX = mybir.AluOpType.max
+
+P = 128
+PACK = 4
+HALF = 128
+HALVES = J // HALF
+NT = N // P
+
+
+def tile_list_crossed_direct_skip_tabled_kernel(
+    tc, xt_words, xt_scales, xo_words, xo_scales, w_words, w_scales, w2_words, w2_scales,
+    wb_words, wb_scales, sx_words, sx_scales, ws_words, ws_scales, tz, offs, offs2, offs3, out,
+):
+    nc = tc.nc
+    with ExitStack() as ctx:
+        keep = ctx.enter_context(tc.tile_pool(name="keep", bufs=1))
+        psum = ctx.enter_context(tc.psum_pool(name="psum", bufs=1))
+
+        def sb(name, shape, dtype):
+            return keep.tile(shape, dtype, name=name, align_bytes=64)
+
+        def words4(ap):
+            return ap[0].rearrange("p n t -> p (n t)").bitcast(I32)
+
+        def load_plane(eng, plane, scales, rs):
+            rows = scales[0].bitcast(I32)
+            view = plane[:].bitcast(I32)
+            for r in rs:
+                eng.dma_start(out=view[r:P:32, :], in_=rows[r:16:4, :])
+
+        idx1 = sb("idx1", [P, J // 16], U16)
+        idx2 = sb("idx2", [P, J // 16], U16)
+        idx3 = sb("idx3", [P, J // 16], U16)
+        xt_w = sb("xt_w", [P, T], U16)
+        xo_w = sb("xo_w", [P, Z], U32)
+        xt_s = sb("xt_s", [P, T], U8)
+        xo_s = sb("xo_s", [P, Z], U8)
+        w_raw = sb("w_raw", [P, R], U32)
+        w2_raw = sb("w2_raw", [P, R], U32)
+        w_sraw = sb("w_sraw", [P, R], U8)
+        w2_sraw = sb("w2_sraw", [P, R], U8)
+        w_c = sb("w_c", [P, R], U32)
+        w2_c = sb("w2_c", [P, R], U32)
+        w_s = sb("w_s", [P, R], U8)
+        w2_s = sb("w2_s", [P, R], U8)
+        wb_w = sb("wb_w", [P, 2 * N], U8)
+        ws_w = sb("ws_w", [P, N], U32)
+        sx_w = sb("sx_w", [P, J], U32)
+        late_s = sb("late_s", [P, 2 * N + J], U8)
+        tz_sb = [sb("tz%d" % n, [P, E], F32) for n in range(NT)]
+        tz_g = sb("tz_g", [P, NT, J], F32)
+
+        nc.gpsimd.memset(xt_s[:].bitcast(I32), 0)
+        for plane in (w_sraw, w2_sraw, xo_s, late_s):
+            nc.vector.memset(plane[:].bitcast(I32), 0)
+
+        late_v = late_s[:].bitcast(I32)
+        nc.sync.dma_start(idx1[:], offs)
+        nc.sync.dma_start(out=w_raw[:].bitcast(I32), in_=words4(w_words))
+        nc.sync.dma_start(out=xt_w[:].bitcast(I32), in_=xt_words[0].bitcast(I32))
+        load_plane(nc.sync, w_sraw, w_scales, range(4))
+        load_plane(nc.sync, xt_s, xt_scales, range(1))
+        load_plane(nc.gpsimd, xt_s, xt_scales, range(1, 4))
+        for c, scales in enumerate((wb_scales, ws_scales, sx_scales)):
+            nc.gpsimd.dma_start(out=late_v[0:16, 64 * c : 64 * (c + 1)], in_=scales[0].bitcast(I32))
+        nc.sync.dma_start(out=w2_raw[:].bitcast(I32), in_=words4(w2_words))
+        load_plane(nc.sync, w2_sraw, w2_scales, range(4))
+        nc.sync.dma_start(out=xo_w[:].bitcast(I32), in_=words4(xo_words))
+        nc.sync.dma_start(idx2[:], offs2)
+        nc.sync.dma_start(out=tz_sb[0][:], in_=tz[0:P, :])
+        load_plane(nc.sync, xo_s, xo_scales, range(4))
+        nc.sync.dma_start(out=tz_sb[1][:], in_=tz[P : 2 * P, :])
+        nc.sync.dma_start(out=ws_w[:].bitcast(I32), in_=words4(ws_words))
+        nc.sync.dma_start(out=sx_w[:].bitcast(I32), in_=words4(sx_words))
+        nc.sync.dma_start(out=wb_w[:].bitcast(I32), in_=wb_words[0].bitcast(I32))
+        nc.sync.dma_start(idx3[:], offs3)
+        for q in range(1, 4):
+            nc.sync.dma_start(out=late_v[32 * q : 32 * q + 4, :], in_=late_v[4 * q : 4 * q + 4, :])
+
+        def deal(copy, dst, src):
+            copy(out=dst[:].rearrange("p (t m) -> p m t", t=PACK), in_=src[:].rearrange("p (m t) -> p m t", t=PACK))
+
+        def half_list(idx, h):
+            return idx[:, h * (HALF // 16) : (h + 1) * (HALF // 16)]
+
+        deal(nc.scalar.copy, w_c, w_raw)
+        deal(nc.vector.tensor_copy, w_s, w_sraw)
+        xt_gw = sb("xt_gw", [P, J], U16)
+        nc.vector.tensor_copy(xt_gw[:], xt_w[:].indirect(idx1[:]))
+        xt_gs = [sb("xt_gs%d" % h, [P, HALF], U8) for h in range(HALVES)]
+        for h in range(HALVES):
+            nc.vector.tensor_copy(xt_gs[h][:], xt_s[:].indirect(half_list(idx1, h)))
+        deal(nc.scalar.copy, w2_c, w2_raw)
+        deal(nc.vector.tensor_copy, w2_s, w2_sraw)
+        xo_gw = [sb("xo_gw%d" % h, [P, HALF], U32) for h in range(HALVES)]
+        xo_gs = [sb("xo_gs%d" % h, [P, HALF], U8) for h in range(HALVES)]
+        for h in range(HALVES):
+            nc.vector.tensor_copy(xo_gs[h][:], xo_s[:].indirect(half_list(idx2, h)))
+            nc.vector.tensor_copy(xo_gw[h][:], xo_w[:].indirect(half_list(idx2, h)))
+
+        a_ps = [psum.tile([P, PACK, HALF], F32, name="a%d" % h) for h in range(HALVES)]
+        b_ps = [psum.tile([P, PACK, HALF], F32, name="b%d" % h) for h in range(HALVES)]
+        p_ps = [psum.tile([P, NT, HALF], F32, name="p%d" % h) for h in range(HALVES)]
+
+        first = (w_c, w_s, E4M3)
+        second = (w2_c, w2_s, E5M2)
+
+        def stage1(bank, weight, rhs, rhs_scale, opens):
+            codes, plane, fmt = weight
+            for t in range(PACK):
+                cols = slice(t * P, (t + 1) * P)
+                nc.tensor.matmul_mx(
+                    out=bank[:, t, :], lhsT=codes[:, cols].bitcast(fmt), lhsT_scale=plane[:, cols],
+                    rhs=rhs, rhs_scale=rhs_scale,
+                    start=(opens and t == 0), stop=(not opens and t == PACK - 1),
+                )
+
+        for banks, weight in ((a_ps, first), (b_ps, second)):
+            for h in range(HALVES):
+                stage1(banks[h], weight, xt_gw[:, h * HALF : (h + 1) * HALF].bitcast(E2M1), xt_gs[h][:], True)
+        for h in range(HALVES):
+            for banks, weight in ((b_ps, first), (a_ps, second)):
+                stage1(banks[h], weight, xo_gw[h][:].bitcast(E4M3), xo_gs[h][:], False)
+
+        for h in range(HALVES):
+            for n in range(NT):
+                nc.tensor.matmul_mx(
+                    out=p_ps[h][:, n, :],
+                    lhsT=ws_w[:, n * P : (n + 1) * P].bitcast(E4M3), lhsT_scale=late_s[:, N + n * P : N + (n + 1) * P],
+                    rhs=sx_w[:, h * HALF : (h + 1) * HALF].bitcast(E4M3),
+                    rhs_scale=late_s[:, 2 * N + h * HALF : 2 * N + (h + 1) * HALF],
+                    start=(n == 0), stop=False,
+                )
+
+        b_sb = [sb("b_sb%d" % h, [P, HALF, PACK], F32) for h in range(HALVES)]
+        hid = [sb("hid%d" % h, [P, HALF, PACK], BF16) for h in range(HALVES)]
+        hid_c = [sb("hid_c%d" % h, [P, HALF], U32) for h in range(HALVES)]
+        hid_s = [sb("hid_s%d" % h, [P, HALF], U8) for h in range(HALVES)]
+        res = [sb("res%d" % h, [P, NT, HALF], F32) for h in range(HALVES)]
+        for h in range(HALVES):
+            nc.scalar.activation(b_sb[h][:], b_ps[h][:].rearrange("p t j -> p j t"), COPY)
+        for n in range(NT):
+            nc.scalar.activation(tz_g[:, n, :], tz_sb[n][:].indirect(idx3[:]), COPY)
+        for h in range(HALVES):
+            nc.vector.tensor_tensor(hid[h][:], a_ps[h][:].rearrange("p t j -> p j t"), b_sb[h][:], MAX)
+            nc.vector.quantize_mx(out=hid_c[h][:].bitcast(E5M2), scales=hid_s[h][:], in_=hid[h][:].rearrange("p j t -> p (j t)"))
+            for n in range(NT):
+                nc.tensor.matmul_mx(
+                    out=p_ps[h][:, n, :],
+                    lhsT=wb_w[:, 2 * n * P : 2 * (n + 1) * P].bitcast(E2M1), lhsT_scale=late_s[:, n * P : (n + 1) * P],
+                    rhs=hid_c[h][:].bitcast(E5M2), rhs_scale=hid_s[h][:],
+                    start=False, stop=(n == NT - 1),
+                )
+        out_v = out.rearrange("(n p) j -> p n j", p=P)
+        for h in range(HALVES):
+            cols = slice(h * HALF, (h + 1) * HALF)
+            nc.vector.tensor_tensor(res[h][:], p_ps[h][:], tz_g[:, :, cols], ADD)
+            nc.sync.dma_start(out=out_v[:, :, cols], in_=res[h][:])

@@ -35,7 +35,7 @@ def tile_list_crossed_direct_skip_tabled_kernel(
         psum = ctx.enter_context(tc.psum_pool(name="psum", bufs=1))
 
         def sb(name, shape, dtype):
-            return keep.tile(shape, dtype, name=name, align_bytes=64)
+            return keep.tile(shape, dtype, name=name, tag=name, align_bytes=64)
 
         def words4(ap):
             return ap[0].rearrange("p n t -> p (n t)").bitcast(I32)
@@ -66,32 +66,30 @@ def tile_list_crossed_direct_skip_tabled_kernel(
         sx_w = sb("sx_w", [P, J], U32)
         late_s = sb("late_s", [P, 2 * N + J], U8)
         tz_sb = [sb("tz%d" % n, [P, E], F32) for n in range(NT)]
-        tz_g = sb("tz_g", [P, NT, J], F32)
 
-        nc.gpsimd.memset(xt_s[:].bitcast(I32), 0)
-        for plane in (w_sraw, w2_sraw, xo_s, late_s):
+        for plane in (w_sraw, xt_s, w2_sraw, late_s, xo_s):
             nc.vector.memset(plane[:].bitcast(I32), 0)
 
         late_v = late_s[:].bitcast(I32)
-        nc.sync.dma_start(idx1[:], offs)
-        nc.sync.dma_start(out=w_raw[:].bitcast(I32), in_=words4(w_words))
-        nc.sync.dma_start(out=xt_w[:].bitcast(I32), in_=xt_words[0].bitcast(I32))
-        load_plane(nc.sync, w_sraw, w_scales, range(4))
-        load_plane(nc.sync, xt_s, xt_scales, range(1))
-        load_plane(nc.gpsimd, xt_s, xt_scales, range(1, 4))
+        nc.gpsimd.dma_start(out=xt_w[:].bitcast(I32), in_=xt_words[0].bitcast(I32))
+        nc.gpsimd.dma_start(out=w_raw[:].bitcast(I32), in_=words4(w_words))
+        nc.gpsimd.dma_start(out=w2_raw[:].bitcast(I32), in_=words4(w2_words))
         for c, scales in enumerate((wb_scales, ws_scales, sx_scales)):
             nc.gpsimd.dma_start(out=late_v[0:16, 64 * c : 64 * (c + 1)], in_=scales[0].bitcast(I32))
-        nc.sync.dma_start(out=w2_raw[:].bitcast(I32), in_=words4(w2_words))
+        nc.sync.dma_start(idx1[:], offs)
+        nc.sync.dma_start(idx2[:], offs2)
+        load_plane(nc.sync, w_sraw, w_scales, range(4))
+        load_plane(nc.scalar, xt_s, xt_scales, range(2))
+        load_plane(nc.sync, xt_s, xt_scales, range(2, 4))
         load_plane(nc.sync, w2_sraw, w2_scales, range(4))
         nc.sync.dma_start(out=xo_w[:].bitcast(I32), in_=words4(xo_words))
-        nc.sync.dma_start(idx2[:], offs2)
-        nc.sync.dma_start(out=tz_sb[0][:], in_=tz[0:P, :])
+        nc.sync.dma_start(idx3[:], offs3)
         load_plane(nc.sync, xo_s, xo_scales, range(4))
-        nc.sync.dma_start(out=tz_sb[1][:], in_=tz[P : 2 * P, :])
+        for n in range(NT):
+            nc.sync.dma_start(out=tz_sb[n][:], in_=tz[n * P : (n + 1) * P, :])
         nc.sync.dma_start(out=ws_w[:].bitcast(I32), in_=words4(ws_words))
         nc.sync.dma_start(out=sx_w[:].bitcast(I32), in_=words4(sx_words))
         nc.sync.dma_start(out=wb_w[:].bitcast(I32), in_=wb_words[0].bitcast(I32))
-        nc.sync.dma_start(idx3[:], offs3)
         for q in range(1, 4):
             nc.sync.dma_start(out=late_v[32 * q : 32 * q + 4, :], in_=late_v[4 * q : 4 * q + 4, :])
 
@@ -101,12 +99,16 @@ def tile_list_crossed_direct_skip_tabled_kernel(
         def half_list(idx, h):
             return idx[:, h * (HALF // 16) : (h + 1) * (HALF // 16)]
 
-        deal(nc.scalar.copy, w_c, w_raw)
+        for u in range(2):
+            nc.scalar.copy(
+                out=w_c[:].rearrange("p (t m) -> p m t", t=PACK)[:, :, 2 * u : 2 * u + 2],
+                in_=w_raw[:].rearrange("p (m t) -> p m t", t=PACK)[:, :, 2 * u : 2 * u + 2],
+            )
         deal(nc.vector.tensor_copy, w_s, w_sraw)
-        xt_gw = sb("xt_gw", [P, J], U16)
-        nc.vector.tensor_copy(xt_gw[:], xt_w[:].indirect(idx1[:]))
+        xt_gw = [sb("xt_gw%d" % h, [P, HALF], U16) for h in range(HALVES)]
         xt_gs = [sb("xt_gs%d" % h, [P, HALF], U8) for h in range(HALVES)]
         for h in range(HALVES):
+            nc.vector.tensor_copy(xt_gw[h][:], xt_w[:].indirect(half_list(idx1, h)))
             nc.vector.tensor_copy(xt_gs[h][:], xt_s[:].indirect(half_list(idx1, h)))
         deal(nc.scalar.copy, w2_c, w2_raw)
         deal(nc.vector.tensor_copy, w2_s, w2_sraw)
@@ -135,7 +137,7 @@ def tile_list_crossed_direct_skip_tabled_kernel(
 
         for banks, weight in ((a_ps, first), (b_ps, second)):
             for h in range(HALVES):
-                stage1(banks[h], weight, xt_gw[:, h * HALF : (h + 1) * HALF].bitcast(E2M1), xt_gs[h][:], True)
+                stage1(banks[h], weight, xt_gw[h][:].bitcast(E2M1), xt_gs[h][:], True)
         for h in range(HALVES):
             for banks, weight in ((b_ps, first), (a_ps, second)):
                 stage1(banks[h], weight, xo_gw[h][:].bitcast(E4M3), xo_gs[h][:], False)
@@ -157,8 +159,10 @@ def tile_list_crossed_direct_skip_tabled_kernel(
         res = [sb("res%d" % h, [P, NT, HALF], F32) for h in range(HALVES)]
         for h in range(HALVES):
             nc.scalar.activation(b_sb[h][:], b_ps[h][:].rearrange("p t j -> p j t"), COPY)
-        for n in range(NT):
-            nc.scalar.activation(tz_g[:, n, :], tz_sb[n][:].indirect(idx3[:]), COPY)
+        tz_g = keep.tile([P, HALVES, NT, HALF], F32, name="tz_g", tag="w2_c", align_bytes=64)
+        for h in range(HALVES):
+            for n in range(NT):
+                nc.scalar.activation(tz_g[:, h, n, :], tz_sb[n][:].indirect(half_list(idx3, h)), COPY)
         for h in range(HALVES):
             nc.vector.tensor_tensor(hid[h][:], a_ps[h][:].rearrange("p t j -> p j t"), b_sb[h][:], MAX)
             nc.vector.quantize_mx(out=hid_c[h][:].bitcast(E5M2), scales=hid_s[h][:], in_=hid[h][:].rearrange("p j t -> p (j t)"))
@@ -172,5 +176,5 @@ def tile_list_crossed_direct_skip_tabled_kernel(
         out_v = out.rearrange("(n p) j -> p n j", p=P)
         for h in range(HALVES):
             cols = slice(h * HALF, (h + 1) * HALF)
-            nc.vector.tensor_tensor(res[h][:], p_ps[h][:], tz_g[:, :, cols], ADD)
+            nc.vector.tensor_tensor(res[h][:], p_ps[h][:], tz_g[:, h, :, :], ADD)
             nc.sync.dma_start(out=out_v[:, :, cols], in_=res[h][:])

@@ -61,34 +61,37 @@ def tile_list_crossed_direct_skip_tabled_kernel(
         w2_c = sb("w2_c", [P, R], U32)
         w_s = sb("w_s", [P, R], U8)
         w2_s = sb("w2_s", [P, R], U8)
+        tz_sb = [sb("tz%d" % n, [P, E], F32) for n in range(NT)]
         wb_w = sb("wb_w", [P, 2 * N], U8)
         ws_w = sb("ws_w", [P, N], U32)
         sx_w = sb("sx_w", [P, J], U32)
         late_s = sb("late_s", [P, 2 * N + J], U8)
-        tz_sb = [sb("tz%d" % n, [P, E], F32) for n in range(NT)]
 
-        for plane in (w_sraw, xt_s, w2_sraw, late_s, xo_s):
+        for plane in (w_sraw, xt_s, w2_sraw, xo_s, late_s):
             nc.vector.memset(plane[:].bitcast(I32), 0)
 
         late_v = late_s[:].bitcast(I32)
-        nc.gpsimd.dma_start(out=xt_w[:].bitcast(I32), in_=xt_words[0].bitcast(I32))
-        nc.gpsimd.dma_start(out=w_raw[:].bitcast(I32), in_=words4(w_words))
+
+        def stage_late(eng, c, scales):
+            eng.dma_start(out=late_v[0:16, 64 * c : 64 * (c + 1)], in_=scales[0].bitcast(I32))
+
+        nc.gpsimd.dma_start(out=xo_w[:].bitcast(I32), in_=words4(xo_words))
         nc.gpsimd.dma_start(out=w2_raw[:].bitcast(I32), in_=words4(w2_words))
-        for c, scales in enumerate((wb_scales, ws_scales, sx_scales)):
-            nc.gpsimd.dma_start(out=late_v[0:16, 64 * c : 64 * (c + 1)], in_=scales[0].bitcast(I32))
+        nc.gpsimd.dma_start(out=ws_w[:].bitcast(I32), in_=words4(ws_words))
+        nc.gpsimd.dma_start(out=sx_w[:].bitcast(I32), in_=words4(sx_words))
         nc.sync.dma_start(idx1[:], offs)
-        nc.sync.dma_start(idx2[:], offs2)
+        nc.sync.dma_start(out=xt_w[:].bitcast(I32), in_=xt_words[0].bitcast(I32))
+        nc.sync.dma_start(out=w_raw[:].bitcast(I32), in_=words4(w_words))
         load_plane(nc.sync, w_sraw, w_scales, range(4))
-        load_plane(nc.scalar, xt_s, xt_scales, range(2))
-        load_plane(nc.sync, xt_s, xt_scales, range(2, 4))
+        load_plane(nc.sync, xt_s, xt_scales, range(4))
         load_plane(nc.sync, w2_sraw, w2_scales, range(4))
-        nc.sync.dma_start(out=xo_w[:].bitcast(I32), in_=words4(xo_words))
-        nc.sync.dma_start(idx3[:], offs3)
+        nc.sync.dma_start(idx2[:], offs2)
         load_plane(nc.sync, xo_s, xo_scales, range(4))
-        for n in range(NT):
-            nc.sync.dma_start(out=tz_sb[n][:], in_=tz[n * P : (n + 1) * P, :])
-        nc.sync.dma_start(out=ws_w[:].bitcast(I32), in_=words4(ws_words))
-        nc.sync.dma_start(out=sx_w[:].bitcast(I32), in_=words4(sx_words))
+        for c, scales in enumerate((wb_scales, ws_scales, sx_scales)):
+            stage_late(nc.sync, c, scales)
+        nc.sync.dma_start(out=tz_sb[0][:], in_=tz[0:P, :])
+        nc.sync.dma_start(idx3[:], offs3)
+        nc.sync.dma_start(out=tz_sb[1][:], in_=tz[P : 2 * P, :])
         nc.sync.dma_start(out=wb_w[:].bitcast(I32), in_=wb_words[0].bitcast(I32))
         for q in range(1, 4):
             nc.sync.dma_start(out=late_v[32 * q : 32 * q + 4, :], in_=late_v[4 * q : 4 * q + 4, :])
@@ -112,15 +115,14 @@ def tile_list_crossed_direct_skip_tabled_kernel(
             nc.vector.tensor_copy(xt_gs[h][:], xt_s[:].indirect(half_list(idx1, h)))
         deal(nc.scalar.copy, w2_c, w2_raw)
         deal(nc.vector.tensor_copy, w2_s, w2_sraw)
-        xo_gw = [sb("xo_gw%d" % h, [P, HALF], U32) for h in range(HALVES)]
-        xo_gs = [sb("xo_gs%d" % h, [P, HALF], U8) for h in range(HALVES)]
+        xo_gw = keep.tile([P, J], U32, name="xo_gw", tag="w2_sraw", align_bytes=64)
+        nc.vector.tensor_copy(xo_gw[:], xo_w[:].indirect(idx2[:]))
+        xo_gs = keep.tile([P, J], U8, name="xo_gs", tag="xo_w", align_bytes=64)
         for h in range(HALVES):
-            nc.vector.tensor_copy(xo_gs[h][:], xo_s[:].indirect(half_list(idx2, h)))
-            nc.vector.tensor_copy(xo_gw[h][:], xo_w[:].indirect(half_list(idx2, h)))
+            nc.vector.tensor_copy(xo_gs[:, h * HALF : (h + 1) * HALF], xo_s[:].indirect(half_list(idx2, h)))
 
-        a_ps = [psum.tile([P, PACK, HALF], F32, name="a%d" % h) for h in range(HALVES)]
-        b_ps = [psum.tile([P, PACK, HALF], F32, name="b%d" % h) for h in range(HALVES)]
-        p_ps = [psum.tile([P, NT, HALF], F32, name="p%d" % h) for h in range(HALVES)]
+        a_ps = [psum.tile([P, PACK, HALF], F32, name="a%d" % h, tag="a%d" % h) for h in range(HALVES)]
+        b_ps = [psum.tile([P, PACK, HALF], F32, name="b%d" % h, tag="b%d" % h) for h in range(HALVES)]
 
         first = (w_c, w_s, E4M3)
         second = (w2_c, w2_s, E5M2)
@@ -135,22 +137,14 @@ def tile_list_crossed_direct_skip_tabled_kernel(
                     start=(opens and t == 0), stop=(not opens and t == PACK - 1),
                 )
 
+        xt_op = [(xt_gw[h][:].bitcast(E2M1), xt_gs[h][:]) for h in range(HALVES)]
+        xo_op = [(xo_gw[:, h * HALF : (h + 1) * HALF].bitcast(E4M3), xo_gs[:, h * HALF : (h + 1) * HALF]) for h in range(HALVES)]
         for banks, weight in ((a_ps, first), (b_ps, second)):
             for h in range(HALVES):
-                stage1(banks[h], weight, xt_gw[h][:].bitcast(E2M1), xt_gs[h][:], True)
+                stage1(banks[h], weight, xt_op[h][0], xt_op[h][1], True)
         for h in range(HALVES):
             for banks, weight in ((b_ps, first), (a_ps, second)):
-                stage1(banks[h], weight, xo_gw[h][:].bitcast(E4M3), xo_gs[h][:], False)
-
-        for h in range(HALVES):
-            for n in range(NT):
-                nc.tensor.matmul_mx(
-                    out=p_ps[h][:, n, :],
-                    lhsT=ws_w[:, n * P : (n + 1) * P].bitcast(E4M3), lhsT_scale=late_s[:, N + n * P : N + (n + 1) * P],
-                    rhs=sx_w[:, h * HALF : (h + 1) * HALF].bitcast(E4M3),
-                    rhs_scale=late_s[:, 2 * N + h * HALF : 2 * N + (h + 1) * HALF],
-                    start=(n == 0), stop=False,
-                )
+                stage1(banks[h], weight, xo_op[h][0], xo_op[h][1], False)
 
         b_sb = [sb("b_sb%d" % h, [P, HALF, PACK], F32) for h in range(HALVES)]
         hid = [sb("hid%d" % h, [P, HALF, PACK], BF16) for h in range(HALVES)]
@@ -159,13 +153,22 @@ def tile_list_crossed_direct_skip_tabled_kernel(
         res = [sb("res%d" % h, [P, NT, HALF], F32) for h in range(HALVES)]
         for h in range(HALVES):
             nc.scalar.activation(b_sb[h][:], b_ps[h][:].rearrange("p t j -> p j t"), COPY)
-        tz_g = keep.tile([P, HALVES, NT, HALF], F32, name="tz_g", tag="w2_c", align_bytes=64)
-        for h in range(HALVES):
-            for n in range(NT):
-                nc.scalar.activation(tz_g[:, h, n, :], tz_sb[n][:].indirect(half_list(idx3, h)), COPY)
-        for h in range(HALVES):
+        tz_g = keep.tile([P, NT, J], F32, name="tz_g", tag="w2_c", align_bytes=64)
+        for n in range(NT):
+            nc.scalar.activation(tz_g[:, n, :], tz_sb[n][:].indirect(idx3[:]), COPY)
+        p_ps = []
+        for h, tag in enumerate(("b1", "a0")):
             nc.vector.tensor_tensor(hid[h][:], a_ps[h][:].rearrange("p t j -> p j t"), b_sb[h][:], MAX)
             nc.vector.quantize_mx(out=hid_c[h][:].bitcast(E5M2), scales=hid_s[h][:], in_=hid[h][:].rearrange("p j t -> p (j t)"))
+            p_ps.append(psum.tile([P, NT, HALF], F32, name="p%d" % h, tag=tag))
+            for n in range(NT):
+                nc.tensor.matmul_mx(
+                    out=p_ps[h][:, n, :],
+                    lhsT=ws_w[:, n * P : (n + 1) * P].bitcast(E4M3), lhsT_scale=late_s[:, N + n * P : N + (n + 1) * P],
+                    rhs=sx_w[:, h * HALF : (h + 1) * HALF].bitcast(E4M3),
+                    rhs_scale=late_s[:, 2 * N + h * HALF : 2 * N + (h + 1) * HALF],
+                    start=(n == 0), stop=False,
+                )
             for n in range(NT):
                 nc.tensor.matmul_mx(
                     out=p_ps[h][:, n, :],
@@ -176,5 +179,6 @@ def tile_list_crossed_direct_skip_tabled_kernel(
         out_v = out.rearrange("(n p) j -> p n j", p=P)
         for h in range(HALVES):
             cols = slice(h * HALF, (h + 1) * HALF)
-            nc.vector.tensor_tensor(res[h][:], p_ps[h][:], tz_g[:, h, :, :], ADD)
+            for n in range(NT):
+                nc.vector.tensor_tensor(res[h][:, n, :], p_ps[h][:, n, :], tz_g[:, n, cols], ADD)
             nc.sync.dma_start(out=out_v[:, :, cols], in_=res[h][:])

from contextlib import ExitStack

import concourse.mybir as mybir

K, T, Z, J, R, N, L, E = 512, 1024, 1024, 256, 512, 256, 512, 1024
FLOPS = 2 * (4 * K * R * J + R * N * J + L * N * J)

F32 = mybir.dt.float32
BF16 = mybir.dt.bfloat16
I32 = mybir.dt.int32
U32 = mybir.dt.uint32
U16 = mybir.dt.uint16
U8 = mybir.dt.uint8
E4M3 = mybir.dt.float8_e4m3fn_x4
E5M2 = mybir.dt.float8_e5m2_x4
E2M1 = mybir.dt.float4_e2m1fn_x4
COPY = mybir.ActivationFunctionType.Copy
ADD = mybir.AluOpType.add
MAX = mybir.AluOpType.max

P = 128
PACK = 4
HALF = 128
HALVES = J // HALF
NT = N // P


def tile_list_crossed_direct_skip_tabled_kernel(
    tc, xt_words, xt_scales, xo_words, xo_scales, w_words, w_scales, w2_words, w2_scales,
    wb_words, wb_scales, sx_words, sx_scales, ws_words, ws_scales, tz, offs, offs2, offs3, out,
):
    nc = tc.nc
    with ExitStack() as ctx:
        keep = ctx.enter_context(tc.tile_pool(name="keep", bufs=1))
        psum = ctx.enter_context(tc.psum_pool(name="psum", bufs=1))

        def sb(name, shape, dtype):
            return keep.tile(shape, dtype, name=name, tag=name, align_bytes=64)

        def words4(ap):
            return ap[0].rearrange("p n t -> p (n t)").bitcast(I32)

        def load_plane(eng, plane, scales, rs):
            rows = scales[0].bitcast(I32)
            view = plane[:].bitcast(I32)
            for r in rs:
                eng.dma_start(out=view[r:P:32, :], in_=rows[r:16:4, :])

        idx1 = sb("idx1", [P, J // 16], U16)
        idx2 = sb("idx2", [P, J // 16], U16)
        idx3 = sb("idx3", [P, J // 16], U16)
        xt_w = sb("xt_w", [P, T], U16)
        xo_w = sb("xo_w", [P, Z], U32)
        xt_s = sb("xt_s", [P, T], U8)
        xo_s = sb("xo_s", [P, Z], U8)
        w_raw = sb("w_raw", [P, R], U32)
        w2_raw = sb("w2_raw", [P, R], U32)
        w_sraw = sb("w_sraw", [P, R], U8)
        w2_sraw = sb("w2_sraw", [P, R], U8)
        w_c = sb("w_c", [P, R], U32)
        w2_c = sb("w2_c", [P, R], U32)
        w_s = sb("w_s", [P, R], U8)
        w2_s = sb("w2_s", [P, R], U8)
        tz_sb = [sb("tz%d" % n, [P, E], F32) for n in range(NT)]
        wb_w = sb("wb_w", [P, 2 * N], U8)
        ws_w = sb("ws_w", [P, N], U32)
        sx_w = sb("sx_w", [P, J], U32)
        late_s = sb("late_s", [P, 2 * N + J], U8)

        for plane in (w_sraw, xt_s, w2_sraw, xo_s, late_s):
            nc.vector.memset(plane[:].bitcast(I32), 0)

        late_v = late_s[:].bitcast(I32)

        def stage_late(eng, c, scales):
            eng.dma_start(out=late_v[0:16, 64 * c : 64 * (c + 1)], in_=scales[0].bitcast(I32))

        nc.gpsimd.dma_start(out=xo_w[:].bitcast(I32), in_=words4(xo_words))
        nc.gpsimd.dma_start(out=w2_raw[:].bitcast(I32), in_=words4(w2_words))
        nc.gpsimd.dma_start(out=ws_w[:].bitcast(I32), in_=words4(ws_words))
        nc.gpsimd.dma_start(out=sx_w[:].bitcast(I32), in_=words4(sx_words))
        nc.sync.dma_start(idx1[:], offs)
        nc.sync.dma_start(out=xt_w[:].bitcast(I32), in_=xt_words[0].bitcast(I32))
        nc.sync.dma_start(out=w_raw[:].bitcast(I32), in_=words4(w_words))
        load_plane(nc.sync, w_sraw, w_scales, range(4))
        load_plane(nc.sync, xt_s, xt_scales, range(4))
        load_plane(nc.sync, w2_sraw, w2_scales, range(4))
        nc.sync.dma_start(idx2[:], offs2)
        load_plane(nc.sync, xo_s, xo_scales, range(4))
        for c, scales in enumerate((wb_scales, ws_scales, sx_scales)):
            stage_late(nc.sync, c, scales)
        nc.sync.dma_start(out=tz_sb[0][:], in_=tz[0:P, :])
        nc.sync.dma_start(idx3[:], offs3)
        nc.sync.dma_start(out=tz_sb[1][:], in_=tz[P : 2 * P, :])
        nc.sync.dma_start(out=wb_w[:].bitcast(I32), in_=wb_words[0].bitcast(I32))
        for q in range(1, 4):
            nc.sync.dma_start(out=late_v[32 * q : 32 * q + 4, :], in_=late_v[4 * q : 4 * q + 4, :])

        def deal(copy, dst, src):
            copy(out=dst[:].rearrange("p (t m) -> p m t", t=PACK), in_=src[:].rearrange("p (m t) -> p m t", t=PACK))

        def half_list(idx, h):
            return idx[:, h * (HALF // 16) : (h + 1) * (HALF // 16)]

        for u in range(2):
            nc.scalar.copy(
                out=w_c[:].rearrange("p (t m) -> p m t", t=PACK)[:, :, 2 * u : 2 * u + 2],
                in_=w_raw[:].rearrange("p (m t) -> p m t", t=PACK)[:, :, 2 * u : 2 * u + 2],
            )
        deal(nc.vector.tensor_copy, w_s, w_sraw)
        xt_gw = [sb("xt_gw%d" % h, [P, HALF], U16) for h in range(HALVES)]
        xt_gs = [sb("xt_gs%d" % h, [P, HALF], U8) for h in range(HALVES)]
        for h in range(HALVES):
            nc.vector.tensor_copy(xt_gw[h][:], xt_w[:].indirect(half_list(idx1, h)))
            nc.vector.tensor_copy(xt_gs[h][:], xt_s[:].indirect(half_list(idx1, h)))
        deal(nc.scalar.copy, w2_c, w2_raw)
        deal(nc.vector.tensor_copy, w2_s, w2_sraw)
        xo_gw = keep.tile([P, J], U32, name="xo_gw", tag="w2_sraw", align_bytes=64)
        nc.vector.tensor_copy(xo_gw[:], xo_w[:].indirect(idx2[:]))
        xo_gs = keep.tile([P, J], U8, name="xo_gs", tag="xo_w", align_bytes=64)
        for h in range(HALVES):
            nc.vector.tensor_copy(xo_gs[:, h * HALF : (h + 1) * HALF], xo_s[:].indirect(half_list(idx2, h)))

        a_ps = [psum.tile([P, PACK, HALF], F32, name="a%d" % h, tag="a%d" % h) for h in range(HALVES)]
        b_ps = [psum.tile([P, PACK, HALF], F32, name="b%d" % h, tag="b%d" % h) for h in range(HALVES)]

        first = (w_c, w_s, E4M3)
        second = (w2_c, w2_s, E5M2)

        def stage1(bank, weight, rhs, rhs_scale, opens):
            codes, plane, fmt = weight
            for t in range(PACK):
                cols = slice(t * P, (t + 1) * P)
                nc.tensor.matmul_mx(
                    out=bank[:, t, :], lhsT=codes[:, cols].bitcast(fmt), lhsT_scale=plane[:, cols],
                    rhs=rhs, rhs_scale=rhs_scale,
                    start=(opens and t == 0), stop=(not opens and t == PACK - 1),
                )

        xt_op = [(xt_gw[h][:].bitcast(E2M1), xt_gs[h][:]) for h in range(HALVES)]
        xo_op = [(xo_gw[:, h * HALF : (h + 1) * HALF].bitcast(E4M3), xo_gs[:, h * HALF : (h + 1) * HALF]) for h in range(HALVES)]
        for banks, weight in ((a_ps, first), (b_ps, second)):
            for h in range(HALVES):
                stage1(banks[h], weight, xt_op[h][0], xt_op[h][1], True)
        for h in range(HALVES):
            for banks, weight in ((b_ps, first), (a_ps, second)):
                stage1(banks[h], weight, xo_op[h][0], xo_op[h][1], False)

        b_sb = [sb("b_sb%d" % h, [P, HALF, PACK], F32) for h in range(HALVES)]
        hid = [sb("hid%d" % h, [P, HALF, PACK], BF16) for h in range(HALVES)]
        hid_c = [sb("hid_c%d" % h, [P, HALF], U32) for h in range(HALVES)]
        hid_s = [sb("hid_s%d" % h, [P, HALF], U8) for h in range(HALVES)]
        res = [sb("res%d" % h, [P, NT, HALF], F32) for h in range(HALVES)]
        for h in range(HALVES):
            nc.scalar.activation(b_sb[h][:], b_ps[h][:].rearrange("p t j -> p j t"), COPY)
        tz_g = keep.tile([P, NT, J], F32, name="tz_g", tag="w2_c", align_bytes=64)
        for n in range(NT):
            nc.scalar.activation(tz_g[:, n, :], tz_sb[n][:].indirect(idx3[:]), COPY)
        p_ps = []
        for h, tag in enumerate(("b1", "a0")):
            nc.vector.tensor_tensor(hid[h][:], a_ps[h][:].rearrange("p t j -> p j t"), b_sb[h][:], MAX)
            nc.vector.quantize_mx(out=hid_c[h][:].bitcast(E5M2), scales=hid_s[h][:], in_=hid[h][:].rearrange("p j t -> p (j t)"))
            p_ps.append(psum.tile([P, NT, HALF], F32, name="p%d" % h, tag=tag))
            for n in range(NT):
                nc.tensor.matmul_mx(
                    out=p_ps[h][:, n, :],
                    lhsT=ws_w[:, n * P : (n + 1) * P].bitcast(E4M3), lhsT_scale=late_s[:, N + n * P : N + (n + 1) * P],
                    rhs=sx_w[:, h * HALF : (h + 1) * HALF].bitcast(E4M3),
                    rhs_scale=late_s[:, 2 * N + h * HALF : 2 * N + (h + 1) * HALF],
                    start=(n == 0), stop=False,
                )
            for n in range(NT):
                nc.tensor.matmul_mx(
                    out=p_ps[h][:, n, :],
                    lhsT=wb_w[:, 2 * n * P : 2 * (n + 1) * P].bitcast(E2M1), lhsT_scale=late_s[:, n * P : (n + 1) * P],
                    rhs=hid_c[h][:].bitcast(E5M2), rhs_scale=hid_s[h][:],
                    start=False, stop=(n == NT - 1),
                )
        out_v = out.rearrange("(n p) j -> p n j", p=P)
        for h in range(HALVES):
            cols = slice(h * HALF, (h + 1) * HALF)
            for n in range(NT):
                nc.vector.tensor_tensor(res[h][:, n, :], p_ps[h][:, n, :], tz_g[:, n, cols], ADD)
            nc.sync.dma_start(out=out_v[:, :, cols], in_=res[h][:])
